import numpy as np
import ml_dtypes


def mxq(x, axis, fmt="e4m3"):
    dtype, down = {"e4m3": (ml_dtypes.float8_e4m3fn, 7), "e5m2": (ml_dtypes.float8_e5m2, 14)}[fmt]
    v = np.moveaxis(np.asarray(x, np.float32).astype(ml_dtypes.bfloat16).astype(np.float64), axis, -1)
    blocks = v.reshape(v.shape[:-1] + (-1, 32))
    amax = np.abs(blocks).max(-1, keepdims=True)
    byte = np.maximum(np.where(amax > 0, np.frexp(amax)[1] - 1 + 127, 0) - down, 1)
    scale = np.exp2(byte - 127.0)
    codes = (blocks / scale).astype(np.float32).astype(dtype).astype(np.float64)
    return np.moveaxis((codes * scale).reshape(v.shape), -1, axis)


WIDE = False


def mx_kscale(k):
    if not WIDE:
        return np.ones(k)
    levels = np.array([10, -10, 5, -5, 0])
    if k % 512:
        return np.exp2(np.random.permutation(np.resize(levels, k // 32))).repeat(32)
    a = np.empty((k // 512, 16))
    for p in range(k // 512):
        a[p, :8] = np.random.permutation(np.resize(levels, 8))
        for g in range(8):
            far = levels[np.abs(levels - a[p, g]) >= 10]
            a[p, g + 8] = far[np.random.randint(len(far))]
    return np.exp2(a.ravel()).repeat(32)


def f64(x):
    return np.asarray(x).astype(np.float64)


def striped(idx):
    return np.tile(idx.reshape(-1, 16).T, (8, 1)).astype(np.uint16)


def unstriped(offs):
    return offs[:16].T.reshape(-1).astype(np.int64)


def striped8(idx):
    return np.concatenate([x.reshape(-1, 16).T for x in idx]).astype(np.uint16)


def runs(offs, k):
    lists = np.stack([offs[16 * r : 16 * r + 16].T.reshape(-1) for r in range(8)]).astype(np.int64)
    return lists[np.arange(k) % 512 // 64]


def pack_weight(w):
    k, n = w.shape
    w = f64(np.asarray(w, np.float32).astype(ml_dtypes.bfloat16)).reshape(k // 32, 32, n)
    amax = np.abs(w).max(1)
    byte = np.clip(np.where(amax > 0, np.frexp(amax)[1] - 1 + 127 - 7, 1), 1, 254)
    scaled = (w * np.exp2(127.0 - byte)[:, None, :]).reshape(k, n).astype(np.float32)
    words = np.ascontiguousarray(scaled.reshape(k // 512, 128, 4, n).transpose(0, 1, 3, 2)).astype(ml_dtypes.float8_e4m3fn).view(np.uint8)
    return words, np.ascontiguousarray(byte.astype(np.uint8).reshape(k // 512, 16, n))


def unpack_weight(words, scales):
    g, p, n, _ = words.shape
    vals = np.ascontiguousarray(words).view(ml_dtypes.float8_e4m3fn).astype(np.float64) * np.repeat(np.exp2(scales.astype(np.float64) - 127.0), 8, axis=1)[..., None]
    return vals.transpose(0, 1, 3, 2).reshape(g * 512, n)


K, T, S, N, H, C, U = 512, 2048, 512, 512, 512, 512, 1024


def setup_inputs():
    n = np.random.standard_normal
    s = mx_kscale(K)[:, None]
    u = mx_kscale(S)
    packed_xT = pack_weight(n((K, T)) * s)
    return {
        "x_words": packed_xT[0],
        "x_scales": packed_xT[1],
        "w1": (n((K, H)) / np.sqrt(K) / s).astype(np.float32),
        "gs": (np.random.uniform(0.5, 1.5, (K, 1)) / s).astype(np.float32),
        "mem": n((C, U)).astype(np.float32),
        "res": (1.5 * n((N, U))).astype(np.float32),
        "gt": (np.random.uniform(0.5, 1.5, (C, 1)) * u[:, None]).astype(np.float32),
        "w2": (n((C, N)) / np.sqrt(C) / u[:, None]).astype(np.float32),
        "offs": striped(np.random.permutation(T)[:S]),
        "n1": striped8(np.stack([np.random.permutation(S) for _ in range(8)])),
        "n2": striped8(np.stack([np.random.permutation(S) for _ in range(8)])),
        "cand": striped(np.random.permutation(T)[:C]),
        "n3": striped8(np.stack([np.random.permutation(U)[:S] for _ in range(8)])),
    }


def reference(x_words, x_scales, w1, gs, mem, res, gt, w2, offs, n1, n2, cand, n3):
    x_cand = unpack_weight(x_words, x_scales)[:, unstriped(cand)]
    xq = unpack_weight(x_words, x_scales)[:, unstriped(offs)]
    y = mxq(f64(w1), 0, "e4m3").T @ xq
    z = f64(gs) * (y - (np.minimum(y[np.arange(H)[:, None], runs(n1, H)], y[np.arange(H)[:, None], runs(n2, H)])))
    s = 0.0625 * ((x_cand.T @ mxq(z, 0, "e4m3")))
    pg = f64(mem).copy()
    pg[np.arange(C)[:, None], runs(n3, C)] = s
    z2 = f64(gt) * pg
    return f64(res) + (mxq(f64(w2), 0, "e4m3").T @ mxq(z2, 0, "e4m3"))

@@ -1,0 +1,188 @@
+from contextlib import ExitStack
+
+import concourse.mybir as mybir
+
+K, T, S, N, H, C, U = 512, 2048, 512, 512, 512, 512, 1024
+FLOPS = 2 * K * H * S + 2 * K * C * S + 2 * C * N * U
+
+F32 = mybir.dt.float32
+BF16 = mybir.dt.bfloat16
+I32 = mybir.dt.int32
+U32 = mybir.dt.uint32
+U16 = mybir.dt.uint16
+U8 = mybir.dt.uint8
+FP8X4 = mybir.dt.float8_e4m3fn_x4
+ALU = mybir.AluOpType
+COPY = mybir.ActivationFunctionType.Copy
+
+P = 128
+PACK = 4
+CHUNK = 128
+WCHUNK = 256
+
+
+def tile_picked_readunderpage_none_p_kernel(
+    tc, x_words, x_scales, w1, gs, mem, res, gt, w2, offs, n1, n2, cand, n3, out
+):
+    nc = tc.nc
+    with ExitStack() as ctx:
+        keep = ctx.enter_context(tc.tile_pool(name="keep", bufs=1))
+        ring = ctx.enter_context(tc.tile_pool(name="ring", bufs=2))
+        psum = ctx.enter_context(tc.psum_pool(name="psum", bufs=1))
+
+        def load_list(src, name):
+            lst = keep.tile([P, src.shape[1]], U16, name=name)
+            nc.sync.dma_start(lst[:], src)
+            return lst
+
+        xs = keep.tile([P, T], U8, name="xs", align_bytes=64)
+        nc.gpsimd.memset(xs[:].bitcast(I32), 0)
+        w1_raw = keep.tile([P, PACK, H], F32, name="w1_raw")
+        nc.sync.dma_start(w1_raw[:], w1.rearrange("(p j) c -> p j c", j=PACK))
+        for q in range(4):
+            nc.sync.dma_start(xs[32 * q : 32 * q + 4, :].bitcast(I32), x_scales[0, 4 * q : 4 * q + 4, :].bitcast(I32))
+        offs_sb = load_list(offs, "offs_sb")
+        xw = keep.tile([P, T], I32, name="xw")
+        nc.sync.dma_start(xw[:], x_words[0].rearrange("p n t -> p (n t)").bitcast(I32))
+        cand_sb = load_list(cand, "cand_sb")
+        n1_sb = load_list(n1, "n1_sb")
+        n2_sb = load_list(n2, "n2_sb")
+        gs_sb = keep.tile([P, PACK], F32, name="gs_sb")
+        nc.sync.dma_start(gs_sb[:], gs.rearrange("(p t) o -> p (t o)", t=PACK))
+        n3_sb = load_list(n3, "n3_sb")
+        gt_sb = keep.tile([P, PACK], F32, name="gt_sb")
+        nc.sync.dma_start(gt_sb[:], gt.rearrange("(p t) o -> p (t o)", t=PACK))
+        mem_rows = mem.rearrange("(p t) u -> t p u", t=PACK)
+        page = []
+        for t in range(PACK):
+            pg = keep.tile([P, U], F32, name="page%d" % t)
+            nc.sync.dma_start(pg[:], mem_rows[t])
+            page.append(pg)
+        w2_raw = keep.tile([P, PACK, N], F32, name="w2_raw")
+        nc.sync.dma_start(w2_raw[:], w2.rearrange("(p j) n -> p j n", j=PACK))
+        res_sb = []
+        res_rows = res.rearrange("(mt p) u -> p mt u", p=P)
+        out_rows = out.rearrange("(mt p) u -> p mt u", p=P)
+        for pair in range(2):
+            r = keep.tile([P, 2, U], F32, name="res%d" % pair)
+            nc.sync.dma_start(r[:], res_rows[:, 2 * pair : 2 * pair + 2, :])
+            res_sb.append(r)
+
+        w1_bf = keep.tile([P, PACK, P, PACK], BF16, name="w1_bf", align_bytes=64)
+        nc.scalar.activation(
+            w1_bf[:].rearrange("p t m j -> p m j t"), w1_raw[:].rearrange("p j (m t) -> p m j t", t=PACK), COPY
+        )
+        xq_s = keep.tile([P, S], U8, name="xq_s", tag="picked_s", align_bytes=64)
+        nc.vector.tensor_copy(xq_s[:], xs[:].indirect(offs_sb[:]))
+        xc_s_raw = keep.tile([P, C], U8, name="xc_s_raw", align_bytes=64)
+        nc.vector.tensor_copy(xc_s_raw[:], xs[:].indirect(cand_sb[:]))
+        w1_c = keep.tile([P, H], U32, name="w1_c", tag="w1_c", align_bytes=64)
+        w1_s = keep.tile([P, H], U8, name="w1_s", align_bytes=64)
+        nc.vector.quantize_mx(w1_c[:].bitcast(FP8X4), w1_s[:], w1_bf[:].rearrange("p t m j -> p (t m j)"))
+        xq_w = keep.tile([P, S], U32, name="xq_w", tag="picked_w", align_bytes=64)
+        nc.vector.tensor_copy(xq_w[:], xw[:].bitcast(U32).indirect(offs_sb[:]))
+        xc_w_raw = keep.tile([P, C], U32, name="xc_w_raw", align_bytes=64)
+        nc.vector.tensor_copy(xc_w_raw[:], xw[:].bitcast(U32).indirect(cand_sb[:]))
+
+        y_sb = []
+        for t in range(PACK):
+            bank = psum.tile([P, S], F32, name="ybank%d" % t, tag="big%d" % t)
+            cols = slice(t * P, (t + 1) * P)
+            nc.tensor.matmul_mx(bank[:], lhsT=w1_c[:, cols].bitcast(FP8X4), lhsT_scale=w1_s[:, cols],
+                                rhs=xq_w[:].bitcast(FP8X4), rhs_scale=xq_s[:], start=True, stop=True)
+            y = keep.tile([P, S], F32, name="y%d" % t)
+            if t < 2:
+                nc.scalar.activation(y[:], bank[:], COPY)
+            else:
+                nc.vector.tensor_copy(y[:], bank[:])
+            y_sb.append(y)
+
+        gy = keep.tile([P, PACK, S], F32, name="gy")
+        for t in range(PACK):
+            nc.gpsimd.tensor_scalar(gy[:, t, :], y_sb[t][:], gs_sb[:, t : t + 1], 0.0, ALU.mult, ALU.add)
+        xc_s = keep.tile([P, C], U8, name="xc_s", tag="picked_s", align_bytes=64)
+        nc.vector.tensor_copy(xc_s[:].rearrange("p (t m) -> p t m", t=PACK), xc_s_raw[:].rearrange("p (m t) -> p t m", t=PACK))
+        xc_w = keep.tile([P, C], U32, name="xc_w", tag="picked_w", align_bytes=64)
+        nc.vector.tensor_copy(xc_w[:].rearrange("p (t m) -> p t m", t=PACK), xc_w_raw[:].rearrange("p (m t) -> p t m", t=PACK))
+
+        n_chunks = S // CHUNK
+        lc = CHUNK // 16
+
+        def score(c):
+            cols = slice(c * CHUNK, (c + 1) * CHUNK)
+            lcols = slice(c * lc, (c + 1) * lc)
+            g1 = ring.tile([P, PACK, CHUNK], F32, name="g1")
+            g2 = ring.tile([P, PACK, CHUNK], F32, name="g2")
+            for t in range(PACK):
+                nc.scalar.activation(g1[:, t, :], y_sb[t][:].indirect(n1_sb[:, lcols]), COPY)
+                nc.scalar.activation(g2[:, t, :], y_sb[t][:].indirect(n2_sb[:, lcols]), COPY)
+            low = ring.tile([P, PACK, CHUNK], F32, name="low")
+            nc.vector.tensor_tensor(low[:], g1[:], g2[:], ALU.min)
+            z_rows = ring.tile([P, PACK, CHUNK], BF16, name="z_rows")
+            for t in range(PACK):
+                nc.vector.scalar_tensor_tensor(z_rows[:, t, :], low[:, t, :], gs_sb[:, t : t + 1], gy[:, t, cols], ALU.mult, ALU.subtract)
+            z_bf = ring.tile([P, CHUNK, PACK], BF16, name="z_bf", align_bytes=64)
+            weave = nc.vector.tensor_copy if c in (0, n_chunks - 1) else nc.scalar.copy
+            weave(z_bf[:].rearrange("p (c i) t -> p c t i", i=4), z_rows[:].rearrange("p t (c i) -> p c t i", i=4))
+            z_c = ring.tile([P, CHUNK], U32, name="z_c", align_bytes=64)
+            z_s = ring.tile([P, CHUNK], U8, name="z_s", align_bytes=64)
+            nc.vector.quantize_mx(z_c[:].bitcast(FP8X4), z_s[:], z_bf[:].rearrange("p c t -> p (c t)"))
+            bank = psum.tile([P, PACK, CHUNK], F32, name="sbank", tag="s%d" % c)
+            for t in range(PACK):
+                tc_cols = slice(t * P, (t + 1) * P)
+                nc.tensor.matmul_mx(bank[:, t, :], lhsT=xc_w[:, tc_cols].bitcast(FP8X4), lhsT_scale=xc_s[:, tc_cols],
+                                    rhs=z_c[:].bitcast(FP8X4), rhs_scale=z_s[:], start=True, stop=True)
+            s_sb = keep.tile([P, PACK, CHUNK], F32, name="s_sb%d" % c)
+            if c == 0:
+                nc.vector.tensor_scalar(s_sb[:], bank[:], -0.0625, None, ALU.mult)
+            else:
+                nc.scalar.activation(s_sb[:], bank[:], COPY, scale=-0.0625)
+            return s_sb
+
+        def put(c, s_sb):
+            lcols = slice(c * lc, (c + 1) * lc)
+            for t in range(PACK):
+                nc.vector.tensor_copy(page[t][:].indirect(n3_sb[:, lcols]), s_sb[:, t, :])
+
+        prev = score(0)
+        for c in range(1, n_chunks):
+            cur = score(c)
+            put(c - 1, prev)
+            prev = cur
+
+        w2_bf = keep.tile([P, N, PACK], BF16, name="w2_bf", align_bytes=64)
+        nc.scalar.activation(w2_bf[:].rearrange("p (c i) j -> p c j i", i=4), w2_raw[:].rearrange("p j (c i) -> p c j i", i=4), COPY)
+        w2_c = keep.tile([P, N], U32, name="w2_c", align_bytes=64)
+        w2_s = keep.tile([P, N], U8, name="w2_s", align_bytes=64)
+        nc.vector.quantize_mx(w2_c[:].bitcast(FP8X4), w2_s[:], w2_bf[:].rearrange("p n j -> p (n j)"))
+
+        put(n_chunks - 1, prev)
+
+        z2_rows = keep.tile([P, PACK, U], BF16, name="z2_rows")
+        for t in (0, 2):
+            nc.scalar.activation(z2_rows[:, t, :], page[t][:], COPY, scale=gt_sb[:, t : t + 1])
+        nc.gpsimd.tensor_scalar(z2_rows[:, 1, :], page[1][:], gt_sb[:, 1:2], 0.0, ALU.mult, ALU.add)
+        t = PACK - 1
+        nc.vector.tensor_scalar(z2_rows[:, t, :], page[t][:], gt_sb[:, t : t + 1], None, ALU.mult)
+
+        for wc in range(U // WCHUNK):
+            cols = slice(wc * WCHUNK, (wc + 1) * WCHUNK)
+            z2_bf = keep.tile([P, WCHUNK, PACK], BF16, name="z2_bf%d" % wc, align_bytes=64)
+            dst = z2_bf[:].rearrange("p (c i) t -> p c t i", i=4)
+            src = z2_rows[:, :, cols].rearrange("p t (c i) -> p c t i", i=4)
+            if wc == 0:
+                nc.vector.tensor_copy(dst, src)
+            else:
+                nc.scalar.copy(dst, src)
+            z2_c = keep.tile([P, WCHUNK], U32, name="z2_c%d" % wc, align_bytes=64)
+            z2_s = keep.tile([P, WCHUNK], U8, name="z2_s%d" % wc, align_bytes=64)
+            nc.vector.quantize_mx(z2_c[:].bitcast(FP8X4), z2_s[:], z2_bf[:].rearrange("p c t -> p (c t)"))
+            for pair in range(2):
+                bank = psum.tile([P, 2, WCHUNK], F32, name="obank", tag="big%d" % ((2 * wc + pair) % 4))
+                for i in range(2):
+                    m_cols = slice((2 * pair + i) * P, (2 * pair + i + 1) * P)
+                    nc.tensor.matmul_mx(bank[:, i, :], lhsT=w2_c[:, m_cols].bitcast(FP8X4), lhsT_scale=w2_s[:, m_cols],
+                                        rhs=z2_c[:].bitcast(FP8X4), rhs_scale=z2_s[:], start=True, stop=True)
+                o = keep.tile([P, 2, WCHUNK], F32, name="o%d_%d" % (wc, pair))
+                nc.vector.tensor_tensor(o[:], bank[:], res_sb[pair][:, :, cols], ALU.add)
+                nc.sync.dma_start(out_rows[:, 2 * pair : 2 * pair + 2, cols], o[:])

@@ -18,7 +18,9 @@ COPY = mybir.ActivationFunctionType.Copy
 P = 128
 PACK = 4
 CHUNK = 128
-WCHUNK = 256
+BANK = 512
+SPLIT = 384
+WIDTHS = (128, 256, 256, 256, 128)
 
 
 def tile_picked_readunderpage_none_p_kernel(
@@ -27,7 +29,6 @@ def tile_picked_readunderpage_none_p_kernel(
     nc = tc.nc
     with ExitStack() as ctx:
         keep = ctx.enter_context(tc.tile_pool(name="keep", bufs=1))
-        ring = ctx.enter_context(tc.tile_pool(name="ring", bufs=2))
         psum = ctx.enter_context(tc.psum_pool(name="psum", bufs=1))
 
         def load_list(src, name):
@@ -60,13 +61,10 @@ def tile_picked_readunderpage_none_p_kernel(
             page.append(pg)
         w2_raw = keep.tile([P, PACK, N], F32, name="w2_raw")
         nc.sync.dma_start(w2_raw[:], w2.rearrange("(p j) n -> p j n", j=PACK))
-        res_sb = []
         res_rows = res.rearrange("(mt p) u -> p mt u", p=P)
         out_rows = out.rearrange("(mt p) u -> p mt u", p=P)
-        for pair in range(2):
-            r = keep.tile([P, 2, U], F32, name="res%d" % pair)
-            nc.sync.dma_start(r[:], res_rows[:, 2 * pair : 2 * pair + 2, :])
-            res_sb.append(r)
+        res_sb = keep.tile([P, N // P, U], F32, name="res_sb")
+        nc.sync.dma_start(res_sb[:], res_rows)
 
         w1_bf = keep.tile([P, PACK, P, PACK], BF16, name="w1_bf", align_bytes=64)
         nc.scalar.activation(
@@ -86,20 +84,20 @@ def tile_picked_readunderpage_none_p_kernel(
 
         y_sb = []
         for t in range(PACK):
-            bank = psum.tile([P, S], F32, name="ybank%d" % t, tag="big%d" % t)
+            bank = psum.tile([P, S], F32, name="ybank%d" % t, tag="bank%d" % t)
             cols = slice(t * P, (t + 1) * P)
             nc.tensor.matmul_mx(bank[:], lhsT=w1_c[:, cols].bitcast(FP8X4), lhsT_scale=w1_s[:, cols],
                                 rhs=xq_w[:].bitcast(FP8X4), rhs_scale=xq_s[:], start=True, stop=True)
             y = keep.tile([P, S], F32, name="y%d" % t)
-            if t < 2:
+            if t == 0:
                 nc.scalar.activation(y[:], bank[:], COPY)
             else:
                 nc.vector.tensor_copy(y[:], bank[:])
             y_sb.append(y)
 
-        gy = keep.tile([P, PACK, S], F32, name="gy")
+        y_all = keep.tile([P, PACK, S], F32, name="y_all")
         for t in range(PACK):
-            nc.gpsimd.tensor_scalar(gy[:, t, :], y_sb[t][:], gs_sb[:, t : t + 1], 0.0, ALU.mult, ALU.add)
+            nc.gpsimd.tensor_scalar(y_all[:, t, :], y_sb[t][:], 1.0, 0.0, ALU.mult, ALU.add)
         xc_s = keep.tile([P, C], U8, name="xc_s", tag="picked_s", align_bytes=64)
         nc.vector.tensor_copy(xc_s[:].rearrange("p (t m) -> p t m", t=PACK), xc_s_raw[:].rearrange("p (m t) -> p t m", t=PACK))
         xc_w = keep.tile([P, C], U32, name="xc_w", tag="picked_w", align_bytes=64)
@@ -108,81 +106,97 @@ def tile_picked_readunderpage_none_p_kernel(
         n_chunks = S // CHUNK
         lc = CHUNK // 16
 
+        def slot(shape, dtype, tag):
+            return keep.tile(shape, dtype, name=tag, tag=tag, align_bytes=64)
+
         def score(c):
             cols = slice(c * CHUNK, (c + 1) * CHUNK)
             lcols = slice(c * lc, (c + 1) * lc)
-            g1 = ring.tile([P, PACK, CHUNK], F32, name="g1")
-            g2 = ring.tile([P, PACK, CHUNK], F32, name="g2")
+            g1 = slot([P, PACK, CHUNK], F32, {2: "z_c0", 3: "z_bf1"}.get(c, "g1_%d" % c))
+            g2 = slot([P, PACK, CHUNK], F32, "g2_%d" % c)
             for t in range(PACK):
                 nc.scalar.activation(g1[:, t, :], y_sb[t][:].indirect(n1_sb[:, lcols]), COPY)
                 nc.scalar.activation(g2[:, t, :], y_sb[t][:].indirect(n2_sb[:, lcols]), COPY)
-            low = ring.tile([P, PACK, CHUNK], F32, name="low")
+            low = slot([P, PACK, CHUNK], F32, "turn%d" % (c - 1) if c >= 2 else "low%d" % c)
             nc.vector.tensor_tensor(low[:], g1[:], g2[:], ALU.min)
-            z_rows = ring.tile([P, PACK, CHUNK], BF16, name="z_rows")
-            for t in range(PACK):
-                nc.vector.scalar_tensor_tensor(z_rows[:, t, :], low[:, t, :], gs_sb[:, t : t + 1], gy[:, t, cols], ALU.mult, ALU.subtract)
-            z_bf = ring.tile([P, CHUNK, PACK], BF16, name="z_bf", align_bytes=64)
-            weave = nc.vector.tensor_copy if c in (0, n_chunks - 1) else nc.scalar.copy
-            weave(z_bf[:].rearrange("p (c i) t -> p c t i", i=4), z_rows[:].rearrange("p t (c i) -> p c t i", i=4))
-            z_c = ring.tile([P, CHUNK], U32, name="z_c", align_bytes=64)
-            z_s = ring.tile([P, CHUNK], U8, name="z_s", align_bytes=64)
+            eng = nc.vector if c == 0 else nc.gpsimd
+            diff = slot([P, PACK, CHUNK], F32, "turn%d" % c)
+            eng.tensor_tensor(diff[:], y_all[:, :, cols], low[:], ALU.subtract)
+            z_bf = slot([P, CHUNK, PACK], BF16, "z_bf%d" % c)
+            eng.tensor_tensor(z_bf[:], diff[:].rearrange("p t c -> p c t"), gs_sb[:].unsqueeze(1).broadcast_to([P, CHUNK, PACK]), ALU.mult)
+            z_c = slot([P, CHUNK], U32, "s_early%d" % (c - 1) if c >= 1 else "z_c0")
+            z_s = slot([P, CHUNK], U8, "z_s%d" % c)
             nc.vector.quantize_mx(z_c[:].bitcast(FP8X4), z_s[:], z_bf[:].rearrange("p c t -> p (c t)"))
-            bank = psum.tile([P, PACK, CHUNK], F32, name="sbank", tag="s%d" % c)
+            bank = psum.tile([P, PACK, CHUNK], F32, name="sbank", tag="bank%d" % (4 + c))
             for t in range(PACK):
-                tc_cols = slice(t * P, (t + 1) * P)
-                nc.tensor.matmul_mx(bank[:, t, :], lhsT=xc_w[:, tc_cols].bitcast(FP8X4), lhsT_scale=xc_s[:, tc_cols],
+                c_cols = slice(t * P, (t + 1) * P)
+                nc.tensor.matmul_mx(bank[:, t, :], lhsT=xc_w[:, c_cols].bitcast(FP8X4), lhsT_scale=xc_s[:, c_cols],
                                     rhs=z_c[:].bitcast(FP8X4), rhs_scale=z_s[:], start=True, stop=True)
-            s_sb = keep.tile([P, PACK, CHUNK], F32, name="s_sb%d" % c)
-            if c == 0:
-                nc.vector.tensor_scalar(s_sb[:], bank[:], -0.0625, None, ALU.mult)
-            else:
-                nc.scalar.activation(s_sb[:], bank[:], COPY, scale=-0.0625)
-            return s_sb
+            return bank
 
-        def put(c, s_sb):
+        def put(c, bank, ts, tag):
             lcols = slice(c * lc, (c + 1) * lc)
-            for t in range(PACK):
-                nc.vector.tensor_copy(page[t][:].indirect(n3_sb[:, lcols]), s_sb[:, t, :])
+            s_sb = slot([P, len(ts), CHUNK], F32, tag)
+            nc.scalar.activation(s_sb[:], bank[:, ts.start : ts.stop, :], COPY, scale=0.0625)
+            for t in ts:
+                nc.vector.tensor_copy(page[t][:].indirect(n3_sb[:, lcols]), s_sb[:, t - ts.start, :])
 
-        prev = score(0)
-        for c in range(1, n_chunks):
-            cur = score(c)
-            put(c - 1, prev)
-            prev = cur
+        early, late = range(0, PACK - 1), range(PACK - 1, PACK)
+        bank = score(0)
+        for c in range(n_chunks - 1):
+            put(c, bank, early, "s_early%d" % c)
+            nxt = score(c + 1)
+            put(c, bank, late, "turn%d" % (c + 1))
+            bank = nxt
 
-        w2_bf = keep.tile([P, N, PACK], BF16, name="w2_bf", align_bytes=64)
-        nc.scalar.activation(w2_bf[:].rearrange("p (c i) j -> p c j i", i=4), w2_raw[:].rearrange("p j (c i) -> p c j i", i=4), COPY)
-        w2_c = keep.tile([P, N], U32, name="w2_c", align_bytes=64)
+        w2_bf = slot([P, N, PACK], BF16, "g2_%d" % (n_chunks - 2))
+        for mt in range(N // P):
+            cols = slice(mt * P, (mt + 1) * P)
+            nc.scalar.activation(
+                w2_bf[:, cols, :].rearrange("p (c i) j -> p c j i", i=4), w2_raw[:, :, cols].rearrange("p j (c i) -> p c j i", i=4), COPY
+            )
+        w2_c = slot([P, N], U32, "turn%d" % (n_chunks - 1))
         w2_s = keep.tile([P, N], U8, name="w2_s", align_bytes=64)
         nc.vector.quantize_mx(w2_c[:].bitcast(FP8X4), w2_s[:], w2_bf[:].rearrange("p n j -> p (n j)"))
 
-        put(n_chunks - 1, prev)
+        put(n_chunks - 1, bank, range(PACK), "s_last")
 
-        z2_rows = keep.tile([P, PACK, U], BF16, name="z2_rows")
-        for t in (0, 2):
-            nc.scalar.activation(z2_rows[:, t, :], page[t][:], COPY, scale=gt_sb[:, t : t + 1])
-        nc.gpsimd.tensor_scalar(z2_rows[:, 1, :], page[1][:], gt_sb[:, 1:2], 0.0, ALU.mult, ALU.add)
-        t = PACK - 1
-        nc.vector.tensor_scalar(z2_rows[:, t, :], page[t][:], gt_sb[:, t : t + 1], None, ALU.mult)
+        parts = (slice(0, SPLIT), slice(SPLIT, U))
+        z2_rows = [keep.tile([P, PACK, part.stop - part.start], BF16, name="z2_rows%d" % i) for i, part in enumerate(parts)]
+        for t in range(PACK):
+            for rows, part in zip(z2_rows, parts):
+                if t == 1:
+                    nc.gpsimd.tensor_scalar(rows[:, t, :], page[t][:, part], gt_sb[:, t : t + 1], 0.0, ALU.mult, ALU.add)
+                elif t == PACK - 1:
+                    nc.vector.tensor_scalar(rows[:, t, :], page[t][:, part], gt_sb[:, t : t + 1], None, ALU.mult)
+                else:
+                    nc.scalar.activation(rows[:, t, :], page[t][:, part], COPY, scale=gt_sb[:, t : t + 1])
 
-        for wc in range(U // WCHUNK):
-            cols = slice(wc * WCHUNK, (wc + 1) * WCHUNK)
-            z2_bf = keep.tile([P, WCHUNK, PACK], BF16, name="z2_bf%d" % wc, align_bytes=64)
-            dst = z2_bf[:].rearrange("p (c i) t -> p c t i", i=4)
-            src = z2_rows[:, :, cols].rearrange("p t (c i) -> p c t i", i=4)
-            if wc == 0:
-                nc.vector.tensor_copy(dst, src)
-            else:
-                nc.scalar.copy(dst, src)
-            z2_c = keep.tile([P, WCHUNK], U32, name="z2_c%d" % wc, align_bytes=64)
-            z2_s = keep.tile([P, WCHUNK], U8, name="z2_s%d" % wc, align_bytes=64)
+        start = 0
+        pieces = []
+        for wc, width in enumerate(WIDTHS):
+            cols = slice(start, start + width)
+            rows = z2_rows[0][:, :, cols] if start < SPLIT else z2_rows[1][:, :, start - SPLIT : start - SPLIT + width]
+            start = start + width
+            z2_bf = keep.tile([P, width, PACK], BF16, name="z2_bf%d" % wc, align_bytes=64)
+            weave = nc.vector.tensor_copy if wc == 0 else nc.scalar.copy
+            weave(z2_bf[:].rearrange("p (c i) t -> p c t i", i=4), rows.rearrange("p t (c i) -> p c t i", i=4))
+            z2_c = keep.tile([P, width], U32, name="z2_c%d" % wc, align_bytes=64)
+            z2_s = keep.tile([P, width], U8, name="z2_s%d" % wc, align_bytes=64)
             nc.vector.quantize_mx(z2_c[:].bitcast(FP8X4), z2_s[:], z2_bf[:].rearrange("p c t -> p (c t)"))
-            for pair in range(2):
-                bank = psum.tile([P, 2, WCHUNK], F32, name="obank", tag="big%d" % ((2 * wc + pair) % 4))
-                for i in range(2):
-                    m_cols = slice((2 * pair + i) * P, (2 * pair + i + 1) * P)
+            pieces.append((cols, z2_c, z2_s))
+
+        n_bank = 0
+        for cols, z2_c, z2_s in pieces:
+            width = cols.stop - cols.start
+            per_bank = BANK // width
+            for m0 in range(0, N // P, per_bank):
+                bank = psum.tile([P, per_bank, width], F32, name="obank", tag="bank%d" % n_bank)
+                for i in range(per_bank):
+                    m_cols = slice((m0 + i) * P, (m0 + i + 1) * P)
                     nc.tensor.matmul_mx(bank[:, i, :], lhsT=w2_c[:, m_cols].bitcast(FP8X4), lhsT_scale=w2_s[:, m_cols],
                                         rhs=z2_c[:].bitcast(FP8X4), rhs_scale=z2_s[:], start=True, stop=True)
-                o = keep.tile([P, 2, WCHUNK], F32, name="o%d_%d" % (wc, pair))
-                nc.vector.tensor_tensor(o[:], bank[:], res_sb[pair][:, :, cols], ALU.add)
-                nc.sync.dma_start(out_rows[:, 2 * pair : 2 * pair + 2, cols], o[:])
+                o = keep.tile([P, per_bank, width], F32, name="o%d" % n_bank)
+                nc.vector.tensor_tensor(o[:], bank[:], res_sb[:, m0 : m0 + per_bank, cols], ALU.add)
+                nc.sync.dma_start(out_rows[:, m0 : m0 + per_bank, cols], o[:])
+                n_bank = n_bank + 1

@@ -17,7 +17,7 @@ COPY = mybir.ActivationFunctionType.Copy
 
 P = 128
 PACK = 4
-CHUNK = 128
+CHUNKS = (128, 128, 256)
 BANK = 512
 SPLIT = 384
 WIDTHS = (128, 256, 256, 256, 128)
@@ -95,79 +95,89 @@ def tile_picked_readunderpage_none_p_kernel(
                 nc.vector.tensor_copy(y[:], bank[:])
             y_sb.append(y)
 
-        y_all = keep.tile([P, PACK, S], F32, name="y_all")
-        for t in range(PACK):
-            nc.gpsimd.tensor_scalar(y_all[:, t, :], y_sb[t][:], 1.0, 0.0, ALU.mult, ALU.add)
         xc_s = keep.tile([P, C], U8, name="xc_s", tag="picked_s", align_bytes=64)
         nc.vector.tensor_copy(xc_s[:].rearrange("p (t m) -> p t m", t=PACK), xc_s_raw[:].rearrange("p (m t) -> p t m", t=PACK))
         xc_w = keep.tile([P, C], U32, name="xc_w", tag="picked_w", align_bytes=64)
         nc.vector.tensor_copy(xc_w[:].rearrange("p (t m) -> p t m", t=PACK), xc_w_raw[:].rearrange("p (m t) -> p t m", t=PACK))
 
-        n_chunks = S // CHUNK
-        lc = CHUNK // 16
-
         def slot(shape, dtype, tag):
             return keep.tile(shape, dtype, name=tag, tag=tag, align_bytes=64)
 
         def score(c):
-            cols = slice(c * CHUNK, (c + 1) * CHUNK)
-            lcols = slice(c * lc, (c + 1) * lc)
-            g1 = slot([P, PACK, CHUNK], F32, {2: "z_c0", 3: "z_bf1"}.get(c, "g1_%d" % c))
-            g2 = slot([P, PACK, CHUNK], F32, "g2_%d" % c)
+            width = CHUNKS[c]
+            cols = slice(sum(CHUNKS[:c]), sum(CHUNKS[: c + 1]))
+            lcols = slice(cols.start // 16, cols.stop // 16)
+            g1 = slot([P, PACK, width], F32, "z_c0" if c == last else "g1_%d" % c)
+            g2 = slot([P, PACK, width], F32, "g2_%d" % c)
             for t in range(PACK):
                 nc.scalar.activation(g1[:, t, :], y_sb[t][:].indirect(n1_sb[:, lcols]), COPY)
                 nc.scalar.activation(g2[:, t, :], y_sb[t][:].indirect(n2_sb[:, lcols]), COPY)
-            low = slot([P, PACK, CHUNK], F32, "turn%d" % (c - 1) if c >= 2 else "low%d" % c)
+            low = slot([P, PACK, width], F32, "low%d" % c)
+            diff = slot([P, PACK, width], F32, "diff%d" % c)
             nc.vector.tensor_tensor(low[:], g1[:], g2[:], ALU.min)
-            eng = nc.vector if c == 0 else nc.gpsimd
-            diff = slot([P, PACK, CHUNK], F32, "turn%d" % c)
-            eng.tensor_tensor(diff[:], y_all[:, :, cols], low[:], ALU.subtract)
-            z_bf = slot([P, CHUNK, PACK], BF16, "z_bf%d" % c)
-            eng.tensor_tensor(z_bf[:], diff[:].rearrange("p t c -> p c t"), gs_sb[:].unsqueeze(1).broadcast_to([P, CHUNK, PACK]), ALU.mult)
-            z_c = slot([P, CHUNK], U32, "s_early%d" % (c - 1) if c >= 1 else "z_c0")
-            z_s = slot([P, CHUNK], U8, "z_s%d" % c)
-            nc.vector.quantize_mx(z_c[:].bitcast(FP8X4), z_s[:], z_bf[:].rearrange("p c t -> p (c t)"))
-            bank = psum.tile([P, PACK, CHUNK], F32, name="sbank", tag="bank%d" % (4 + c))
             for t in range(PACK):
-                c_cols = slice(t * P, (t + 1) * P)
-                nc.tensor.matmul_mx(bank[:, t, :], lhsT=xc_w[:, c_cols].bitcast(FP8X4), lhsT_scale=xc_s[:, c_cols],
-                                    rhs=z_c[:].bitcast(FP8X4), rhs_scale=z_s[:], start=True, stop=True)
-            return bank
+                nc.vector.tensor_tensor(diff[:, t, :], y_sb[t][:, cols], low[:, t, :], ALU.subtract)
+            z_bf = slot([P, width, PACK], BF16, "z_bf%d" % c)
+            if c < last:
+                nc.vector.tensor_tensor(z_bf[:], diff[:].rearrange("p t c -> p c t"), gs_sb[:].unsqueeze(1).broadcast_to([P, width, PACK]), ALU.mult)
+            else:
+                z_rows = slot([P, PACK, width], BF16, "z_rows")
+                for t in range(PACK):
+                    nc.scalar.activation(z_rows[:, t, :], diff[:, t, :], COPY, scale=gs_sb[:, t : t + 1])
+                nc.scalar.copy(z_bf[:].rearrange("p (c i) t -> p c t i", i=4), z_rows[:].rearrange("p t (c i) -> p c t i", i=4))
+            z_c = slot([P, width], U32, "z_c%d" % c)
+            z_s = slot([P, width], U8, "z_s%d" % c)
+            nc.vector.quantize_mx(z_c[:].bitcast(FP8X4), z_s[:], z_bf[:].rearrange("p c t -> p (c t)"))
+            per_bank = BANK // width
+            banks = []
+            for t0 in range(0, PACK, per_bank):
+                bank = psum.tile([P, per_bank, width], F32, name="sbank", tag="bank%d" % (4 + c + t0 // per_bank))
+                for i in range(per_bank):
+                    c_cols = slice((t0 + i) * P, (t0 + i + 1) * P)
+                    nc.tensor.matmul_mx(bank[:, i, :], lhsT=xc_w[:, c_cols].bitcast(FP8X4), lhsT_scale=xc_s[:, c_cols],
+                                        rhs=z_c[:].bitcast(FP8X4), rhs_scale=z_s[:], start=True, stop=True)
+                banks.append(bank)
+            return banks, lcols
 
-        def put(c, bank, ts, tag):
-            lcols = slice(c * lc, (c + 1) * lc)
-            s_sb = slot([P, len(ts), CHUNK], F32, tag)
-            nc.scalar.activation(s_sb[:], bank[:, ts.start : ts.stop, :], COPY, scale=0.0625)
-            for t in ts:
-                nc.vector.tensor_copy(page[t][:].indirect(n3_sb[:, lcols]), s_sb[:, t - ts.start, :])
+        def empty(values, tag):
+            s_sb = slot(list(values.shape), F32, tag)
+            nc.scalar.activation(s_sb[:], values, COPY, scale=0.0625)
+            return s_sb
 
-        early, late = range(0, PACK - 1), range(PACK - 1, PACK)
-        bank = score(0)
-        for c in range(n_chunks - 1):
-            put(c, bank, early, "s_early%d" % c)
-            nxt = score(c + 1)
-            put(c, bank, late, "turn%d" % (c + 1))
-            bank = nxt
+        def scatter(s_sb, t0, lcols):
+            for i in range(s_sb.shape[1]):
+                nc.vector.tensor_copy(page[t0 + i][:].indirect(n3_sb[:, lcols]), s_sb[:, i, :])
 
-        w2_bf = slot([P, N, PACK], BF16, "g2_%d" % (n_chunks - 2))
+        last = len(CHUNKS) - 1
+        banks0, list0 = score(0)
+        s0 = empty(banks0[0][:], "s0")
+        banks1, list1 = score(1)
+        scatter(s0, 0, list0)
+        banks2, list2 = score(2)
+        s1_early = empty(banks1[0][:, 0 : PACK - 1, :], "g2_2")
+        s1_late = empty(banks1[0][:, PACK - 1 : PACK, :], "z_rows")
+        s2 = [empty(bank[:], "s2_%d" % i) for i, bank in enumerate(banks2)]
+        scatter(s1_early, 0, list1)
+        scatter(s1_late, PACK - 1, list1)
+
+        w2_bf = slot([P, N, PACK], BF16, "g2_1")
         for mt in range(N // P):
             cols = slice(mt * P, (mt + 1) * P)
             nc.scalar.activation(
                 w2_bf[:, cols, :].rearrange("p (c i) j -> p c j i", i=4), w2_raw[:, :, cols].rearrange("p j (c i) -> p c j i", i=4), COPY
             )
-        w2_c = slot([P, N], U32, "turn%d" % (n_chunks - 1))
+        w2_c = slot([P, N], U32, "z_bf2")
         w2_s = keep.tile([P, N], U8, name="w2_s", align_bytes=64)
         nc.vector.quantize_mx(w2_c[:].bitcast(FP8X4), w2_s[:], w2_bf[:].rearrange("p n j -> p (n j)"))
 
-        put(n_chunks - 1, bank, range(PACK), "s_last")
+        for i, s_sb in enumerate(s2):
+            scatter(s_sb, 2 * i, list2)
 
         parts = (slice(0, SPLIT), slice(SPLIT, U))
         z2_rows = [keep.tile([P, PACK, part.stop - part.start], BF16, name="z2_rows%d" % i) for i, part in enumerate(parts)]
         for t in range(PACK):
             for rows, part in zip(z2_rows, parts):
-                if t == 1:
-                    nc.gpsimd.tensor_scalar(rows[:, t, :], page[t][:, part], gt_sb[:, t : t + 1], 0.0, ALU.mult, ALU.add)
-                elif t == PACK - 1:
+                if t == PACK - 1:
                     nc.vector.tensor_scalar(rows[:, t, :], page[t][:, part], gt_sb[:, t : t + 1], None, ALU.mult)
                 else:
                     nc.scalar.activation(rows[:, t, :], page[t][:, part], COPY, scale=gt_sb[:, t : t + 1])

@@ -74,7 +74,7 @@ def tile_picked_readunderpage_none_p_kernel(
         nc.vector.tensor_copy(xq_s[:], xs[:].indirect(offs_sb[:]))
         xc_s_raw = keep.tile([P, C], U8, name="xc_s_raw", align_bytes=64)
         nc.vector.tensor_copy(xc_s_raw[:], xs[:].indirect(cand_sb[:]))
-        w1_c = keep.tile([P, H], U32, name="w1_c", tag="w1_c", align_bytes=64)
+        w1_c = keep.tile([P, H], U32, name="w1_c", align_bytes=64)
         w1_s = keep.tile([P, H], U8, name="w1_s", align_bytes=64)
         nc.vector.quantize_mx(w1_c[:].bitcast(FP8X4), w1_s[:], w1_bf[:].rearrange("p t m j -> p (t m j)"))
         xq_w = keep.tile([P, S], U32, name="xq_w", tag="picked_w", align_bytes=64)
@@ -95,6 +95,9 @@ def tile_picked_readunderpage_none_p_kernel(
                 nc.vector.tensor_copy(y[:], bank[:])
             y_sb.append(y)
 
+        gy = keep.tile([P, PACK, S], F32, name="gy")
+        for t in range(PACK):
+            nc.gpsimd.tensor_scalar(gy[:, t, :], y_sb[t][:], gs_sb[:, t : t + 1], 0.0, ALU.mult, ALU.add)
         xc_s = keep.tile([P, C], U8, name="xc_s", tag="picked_s", align_bytes=64)
         nc.vector.tensor_copy(xc_s[:].rearrange("p (t m) -> p t m", t=PACK), xc_s_raw[:].rearrange("p (m t) -> p t m", t=PACK))
         xc_w = keep.tile([P, C], U32, name="xc_w", tag="picked_w", align_bytes=64)
@@ -113,18 +116,13 @@ def tile_picked_readunderpage_none_p_kernel(
                 nc.scalar.activation(g1[:, t, :], y_sb[t][:].indirect(n1_sb[:, lcols]), COPY)
                 nc.scalar.activation(g2[:, t, :], y_sb[t][:].indirect(n2_sb[:, lcols]), COPY)
             low = slot([P, PACK, width], F32, "low%d" % c)
-            diff = slot([P, PACK, width], F32, "diff%d" % c)
             nc.vector.tensor_tensor(low[:], g1[:], g2[:], ALU.min)
+            z_rows = slot([P, PACK, width], BF16, "z_rows%d" % c)
             for t in range(PACK):
-                nc.vector.tensor_tensor(diff[:, t, :], y_sb[t][:, cols], low[:, t, :], ALU.subtract)
+                nc.vector.scalar_tensor_tensor(z_rows[:, t, :], low[:, t, :], gs_sb[:, t : t + 1], gy[:, t, cols], ALU.mult, ALU.subtract)
             z_bf = slot([P, width, PACK], BF16, "z_bf%d" % c)
-            if c < last:
-                nc.vector.tensor_tensor(z_bf[:], diff[:].rearrange("p t c -> p c t"), gs_sb[:].unsqueeze(1).broadcast_to([P, width, PACK]), ALU.mult)
-            else:
-                z_rows = slot([P, PACK, width], BF16, "z_rows")
-                for t in range(PACK):
-                    nc.scalar.activation(z_rows[:, t, :], diff[:, t, :], COPY, scale=gs_sb[:, t : t + 1])
-                nc.scalar.copy(z_bf[:].rearrange("p (c i) t -> p c t i", i=4), z_rows[:].rearrange("p t (c i) -> p c t i", i=4))
+            weave = nc.scalar.copy if c == last else nc.vector.tensor_copy
+            weave(z_bf[:].rearrange("p (c i) t -> p c t i", i=4), z_rows[:].rearrange("p t (c i) -> p c t i", i=4))
             z_c = slot([P, width], U32, "z_c%d" % c)
             z_s = slot([P, width], U8, "z_s%d" % c)
             nc.vector.quantize_mx(z_c[:].bitcast(FP8X4), z_s[:], z_bf[:].rearrange("p c t -> p (c t)"))
@@ -141,7 +139,7 @@ def tile_picked_readunderpage_none_p_kernel(
 
         def empty(values, tag):
             s_sb = slot(list(values.shape), F32, tag)
-            nc.scalar.activation(s_sb[:], values, COPY, scale=0.0625)
+            nc.scalar.activation(s_sb[:], values, COPY, scale=-0.0625)
             return s_sb
 
         def scatter(s_sb, t0, lcols):
@@ -154,11 +152,15 @@ def tile_picked_readunderpage_none_p_kernel(
         banks1, list1 = score(1)
         scatter(s0, 0, list0)
         banks2, list2 = score(2)
-        s1_early = empty(banks1[0][:, 0 : PACK - 1, :], "g2_2")
-        s1_late = empty(banks1[0][:, PACK - 1 : PACK, :], "z_rows")
-        s2 = [empty(bank[:], "s2_%d" % i) for i, bank in enumerate(banks2)]
+        s1_early = empty(banks1[0][:, 0:2, :], "g2_2")
+        s1_late = empty(banks1[0][:, 2:4, :], "z_rows2")
+        s2_01 = empty(banks2[0][:], "s2_01")
+        s2_2 = empty(banks2[1][:, 0:1, :], "s2_2")
+        s2_3 = empty(banks2[1][:, 1:2, :], "s2_3")
         scatter(s1_early, 0, list1)
-        scatter(s1_late, PACK - 1, list1)
+        scatter(s1_late, 2, list1)
+        scatter(s2_01, 0, list2)
+        scatter(s2_2, 2, list2)
 
         w2_bf = slot([P, N, PACK], BF16, "g2_1")
         for mt in range(N // P):
@@ -166,12 +168,16 @@ def tile_picked_readunderpage_none_p_kernel(
             nc.scalar.activation(
                 w2_bf[:, cols, :].rearrange("p (c i) j -> p c j i", i=4), w2_raw[:, :, cols].rearrange("p j (c i) -> p c j i", i=4), COPY
             )
-        w2_c = slot([P, N], U32, "z_bf2")
+        w2_c = slot([P, N], U32, "s2_2")
         w2_s = keep.tile([P, N], U8, name="w2_s", align_bytes=64)
         nc.vector.quantize_mx(w2_c[:].bitcast(FP8X4), w2_s[:], w2_bf[:].rearrange("p n j -> p (n j)"))
 
-        for i, s_sb in enumerate(s2):
-            scatter(s_sb, 2 * i, list2)
+        warm = psum.tile([P, BANK], F32, name="warm", tag="bank7")
+        for i in range(3):
+            nc.tensor.matmul_mx(warm[:], lhsT=w2_c[:, 0:P].bitcast(FP8X4), lhsT_scale=w2_s[:, 0:P],
+                                rhs=xc_w[:].bitcast(FP8X4), rhs_scale=xc_s[:], start=True, stop=True)
+
+        scatter(s2_3, 3, list2)
 
         parts = (slice(0, SPLIT), slice(SPLIT, U))
         z2_rows = [keep.tile([P, PACK, part.stop - part.start], BF16, name="z2_rows%d" % i) for i, part in enumerate(parts)]
@@ -188,7 +194,7 @@ def tile_picked_readunderpage_none_p_kernel(
             cols = slice(start, start + width)
             rows = z2_rows[0][:, :, cols] if start < SPLIT else z2_rows[1][:, :, start - SPLIT : start - SPLIT + width]
             start = start + width
-            z2_bf = keep.tile([P, width, PACK], BF16, name="z2_bf%d" % wc, align_bytes=64)
+            z2_bf = slot([P, width, PACK], BF16, "z2_bf%d" % wc)
             weave = nc.vector.tensor_copy if wc == 0 else nc.scalar.copy
             weave(z2_bf[:].rearrange("p (c i) t -> p c t i", i=4), rows.rearrange("p t (c i) -> p c t i", i=4))
             z2_c = keep.tile([P, width], U32, name="z2_c%d" % wc, align_bytes=64)
@@ -206,7 +212,7 @@ def tile_picked_readunderpage_none_p_kernel(
                     m_cols = slice((m0 + i) * P, (m0 + i + 1) * P)
                     nc.tensor.matmul_mx(bank[:, i, :], lhsT=w2_c[:, m_cols].bitcast(FP8X4), lhsT_scale=w2_s[:, m_cols],
                                         rhs=z2_c[:].bitcast(FP8X4), rhs_scale=z2_s[:], start=True, stop=True)
-                o = keep.tile([P, per_bank, width], F32, name="o%d" % n_bank)
+                o = slot([P, per_bank, width], F32, "z2_bf%d" % (n_bank + 1) if n_bank + 1 < len(WIDTHS) else "o%d" % n_bank)
                 nc.vector.tensor_tensor(o[:], bank[:], res_sb[:, m0 : m0 + per_bank, cols], ALU.add)
                 nc.sync.dma_start(out_rows[:, m0 : m0 + per_bank, cols], o[:])
                 n_bank = n_bank + 1

@@ -19,8 +19,8 @@ P = 128
 PACK = 4
 CHUNKS = (128, 128, 256)
 BANK = 512
-SPLIT = 384
-WIDTHS = (128, 256, 256, 256, 128)
+SPLIT = 256
+WIDTHS = (128, 128, 256, 512)
 
 
 def tile_picked_readunderpage_none_p_kernel(
@@ -154,13 +154,9 @@ def tile_picked_readunderpage_none_p_kernel(
         banks2, list2 = score(2)
         s1_early = empty(banks1[0][:, 0:2, :], "g2_2")
         s1_late = empty(banks1[0][:, 2:4, :], "z_rows2")
-        s2_01 = empty(banks2[0][:], "s2_01")
-        s2_2 = empty(banks2[1][:, 0:1, :], "s2_2")
-        s2_3 = empty(banks2[1][:, 1:2, :], "s2_3")
+        s2 = [empty(bank[:], "s2_%d" % i) for i, bank in enumerate(banks2)]
         scatter(s1_early, 0, list1)
         scatter(s1_late, 2, list1)
-        scatter(s2_01, 0, list2)
-        scatter(s2_2, 2, list2)
 
         w2_bf = slot([P, N, PACK], BF16, "g2_1")
         for mt in range(N // P):
@@ -168,16 +164,12 @@ def tile_picked_readunderpage_none_p_kernel(
             nc.scalar.activation(
                 w2_bf[:, cols, :].rearrange("p (c i) j -> p c j i", i=4), w2_raw[:, :, cols].rearrange("p j (c i) -> p c j i", i=4), COPY
             )
-        w2_c = slot([P, N], U32, "s2_2")
+        w2_c = slot([P, N], U32, "z_bf2")
         w2_s = keep.tile([P, N], U8, name="w2_s", align_bytes=64)
         nc.vector.quantize_mx(w2_c[:].bitcast(FP8X4), w2_s[:], w2_bf[:].rearrange("p n j -> p (n j)"))
 
-        warm = psum.tile([P, BANK], F32, name="warm", tag="bank7")
-        for i in range(3):
-            nc.tensor.matmul_mx(warm[:], lhsT=w2_c[:, 0:P].bitcast(FP8X4), lhsT_scale=w2_s[:, 0:P],
-                                rhs=xc_w[:].bitcast(FP8X4), rhs_scale=xc_s[:], start=True, stop=True)
-
-        scatter(s2_3, 3, list2)
+        for i, s_sb in enumerate(s2):
+            scatter(s_sb, 2 * i, list2)
 
         parts = (slice(0, SPLIT), slice(SPLIT, U))
         z2_rows = [keep.tile([P, PACK, part.stop - part.start], BF16, name="z2_rows%d" % i) for i, part in enumerate(parts)]

from contextlib import ExitStack

import concourse.mybir as mybir

K, T, S, N, H, C, U = 512, 2048, 512, 512, 512, 512, 1024
FLOPS = 2 * K * H * S + 2 * K * C * S + 2 * C * N * U

F32 = mybir.dt.float32
BF16 = mybir.dt.bfloat16
I32 = mybir.dt.int32
U32 = mybir.dt.uint32
U16 = mybir.dt.uint16
U8 = mybir.dt.uint8
FP8X4 = mybir.dt.float8_e4m3fn_x4
ALU = mybir.AluOpType
COPY = mybir.ActivationFunctionType.Copy

P = 128
PACK = 4
CHUNKS = (128, 128, 256)
BANK = 512
SPLIT = 256
WIDTHS = (128, 128, 256, 512)


def tile_picked_readunderpage_none_p_kernel(
    tc, x_words, x_scales, w1, gs, mem, res, gt, w2, offs, n1, n2, cand, n3, out
):
    nc = tc.nc
    with ExitStack() as ctx:
        keep = ctx.enter_context(tc.tile_pool(name="keep", bufs=1))
        psum = ctx.enter_context(tc.psum_pool(name="psum", bufs=1))

        def load_list(src, name):
            lst = keep.tile([P, src.shape[1]], U16, name=name)
            nc.sync.dma_start(lst[:], src)
            return lst

        xs = keep.tile([P, T], U8, name="xs", align_bytes=64)
        nc.gpsimd.memset(xs[:].bitcast(I32), 0)
        w1_raw = keep.tile([P, PACK, H], F32, name="w1_raw")
        nc.sync.dma_start(w1_raw[:], w1.rearrange("(p j) c -> p j c", j=PACK))
        for q in range(4):
            nc.sync.dma_start(xs[32 * q : 32 * q + 4, :].bitcast(I32), x_scales[0, 4 * q : 4 * q + 4, :].bitcast(I32))
        offs_sb = load_list(offs, "offs_sb")
        xw = keep.tile([P, T], I32, name="xw")
        nc.sync.dma_start(xw[:], x_words[0].rearrange("p n t -> p (n t)").bitcast(I32))
        cand_sb = load_list(cand, "cand_sb")
        n1_sb = load_list(n1, "n1_sb")
        n2_sb = load_list(n2, "n2_sb")
        gs_sb = keep.tile([P, PACK], F32, name="gs_sb")
        nc.sync.dma_start(gs_sb[:], gs.rearrange("(p t) o -> p (t o)", t=PACK))
        n3_sb = load_list(n3, "n3_sb")
        gt_sb = keep.tile([P, PACK], F32, name="gt_sb")
        nc.sync.dma_start(gt_sb[:], gt.rearrange("(p t) o -> p (t o)", t=PACK))
        mem_rows = mem.rearrange("(p t) u -> t p u", t=PACK)
        page = []
        for t in range(PACK):
            pg = keep.tile([P, U], F32, name="page%d" % t)
            nc.sync.dma_start(pg[:], mem_rows[t])
            page.append(pg)
        w2_raw = keep.tile([P, PACK, N], F32, name="w2_raw")
        nc.sync.dma_start(w2_raw[:], w2.rearrange("(p j) n -> p j n", j=PACK))
        res_rows = res.rearrange("(mt p) u -> p mt u", p=P)
        out_rows = out.rearrange("(mt p) u -> p mt u", p=P)
        res_sb = keep.tile([P, N // P, U], F32, name="res_sb")
        nc.sync.dma_start(res_sb[:], res_rows)

        w1_bf = keep.tile([P, PACK, P, PACK], BF16, name="w1_bf", align_bytes=64)
        nc.scalar.activation(
            w1_bf[:].rearrange("p t m j -> p m j t"), w1_raw[:].rearrange("p j (m t) -> p m j t", t=PACK), COPY
        )
        xq_s = keep.tile([P, S], U8, name="xq_s", tag="picked_s", align_bytes=64)
        nc.vector.tensor_copy(xq_s[:], xs[:].indirect(offs_sb[:]))
        xc_s_raw = keep.tile([P, C], U8, name="xc_s_raw", align_bytes=64)
        nc.vector.tensor_copy(xc_s_raw[:], xs[:].indirect(cand_sb[:]))
        w1_c = keep.tile([P, H], U32, name="w1_c", align_bytes=64)
        w1_s = keep.tile([P, H], U8, name="w1_s", align_bytes=64)
        nc.vector.quantize_mx(w1_c[:].bitcast(FP8X4), w1_s[:], w1_bf[:].rearrange("p t m j -> p (t m j)"))
        xq_w = keep.tile([P, S], U32, name="xq_w", tag="picked_w", align_bytes=64)
        nc.vector.tensor_copy(xq_w[:], xw[:].bitcast(U32).indirect(offs_sb[:]))
        xc_w_raw = keep.tile([P, C], U32, name="xc_w_raw", align_bytes=64)
        nc.vector.tensor_copy(xc_w_raw[:], xw[:].bitcast(U32).indirect(cand_sb[:]))

        y_sb = []
        for t in range(PACK):
            bank = psum.tile([P, S], F32, name="ybank%d" % t, tag="bank%d" % t)
            cols = slice(t * P, (t + 1) * P)
            nc.tensor.matmul_mx(bank[:], lhsT=w1_c[:, cols].bitcast(FP8X4), lhsT_scale=w1_s[:, cols],
                                rhs=xq_w[:].bitcast(FP8X4), rhs_scale=xq_s[:], start=True, stop=True)
            y = keep.tile([P, S], F32, name="y%d" % t)
            if t == 0:
                nc.scalar.activation(y[:], bank[:], COPY)
            else:
                nc.vector.tensor_copy(y[:], bank[:])
            y_sb.append(y)

        gy = keep.tile([P, PACK, S], F32, name="gy")
        for t in range(PACK):
            nc.gpsimd.tensor_scalar(gy[:, t, :], y_sb[t][:], gs_sb[:, t : t + 1], 0.0, ALU.mult, ALU.add)
        xc_s = keep.tile([P, C], U8, name="xc_s", tag="picked_s", align_bytes=64)
        nc.vector.tensor_copy(xc_s[:].rearrange("p (t m) -> p t m", t=PACK), xc_s_raw[:].rearrange("p (m t) -> p t m", t=PACK))
        xc_w = keep.tile([P, C], U32, name="xc_w", tag="picked_w", align_bytes=64)
        nc.vector.tensor_copy(xc_w[:].rearrange("p (t m) -> p t m", t=PACK), xc_w_raw[:].rearrange("p (m t) -> p t m", t=PACK))

        def slot(shape, dtype, tag):
            return keep.tile(shape, dtype, name=tag, tag=tag, align_bytes=64)

        def score(c):
            width = CHUNKS[c]
            cols = slice(sum(CHUNKS[:c]), sum(CHUNKS[: c + 1]))
            lcols = slice(cols.start // 16, cols.stop // 16)
            g1 = slot([P, PACK, width], F32, "z_c0" if c == last else "g1_%d" % c)
            g2 = slot([P, PACK, width], F32, "g2_%d" % c)
            for t in range(PACK):
                nc.scalar.activation(g1[:, t, :], y_sb[t][:].indirect(n1_sb[:, lcols]), COPY)
                nc.scalar.activation(g2[:, t, :], y_sb[t][:].indirect(n2_sb[:, lcols]), COPY)
            low = slot([P, PACK, width], F32, "low%d" % c)
            nc.vector.tensor_tensor(low[:], g1[:], g2[:], ALU.min)
            z_rows = slot([P, PACK, width], BF16, "z_rows%d" % c)
            for t in range(PACK):
                nc.vector.scalar_tensor_tensor(z_rows[:, t, :], low[:, t, :], gs_sb[:, t : t + 1], gy[:, t, cols], ALU.mult, ALU.subtract)
            z_bf = slot([P, width, PACK], BF16, "z_bf%d" % c)
            weave = nc.scalar.copy if c == last else nc.vector.tensor_copy
            weave(z_bf[:].rearrange("p (c i) t -> p c t i", i=4), z_rows[:].rearrange("p t (c i) -> p c t i", i=4))
            z_c = slot([P, width], U32, "z_c%d" % c)
            z_s = slot([P, width], U8, "z_s%d" % c)
            nc.vector.quantize_mx(z_c[:].bitcast(FP8X4), z_s[:], z_bf[:].rearrange("p c t -> p (c t)"))
            per_bank = BANK // width
            banks = []
            for t0 in range(0, PACK, per_bank):
                bank = psum.tile([P, per_bank, width], F32, name="sbank", tag="bank%d" % (4 + c + t0 // per_bank))
                for i in range(per_bank):
                    c_cols = slice((t0 + i) * P, (t0 + i + 1) * P)
                    nc.tensor.matmul_mx(bank[:, i, :], lhsT=xc_w[:, c_cols].bitcast(FP8X4), lhsT_scale=xc_s[:, c_cols],
                                        rhs=z_c[:].bitcast(FP8X4), rhs_scale=z_s[:], start=True, stop=True)
                banks.append(bank)
            return banks, lcols

        def empty(values, tag):
            s_sb = slot(list(values.shape), F32, tag)
            nc.scalar.activation(s_sb[:], values, COPY, scale=-0.0625)
            return s_sb

        def scatter(s_sb, t0, lcols):
            for i in range(s_sb.shape[1]):
                nc.vector.tensor_copy(page[t0 + i][:].indirect(n3_sb[:, lcols]), s_sb[:, i, :])

        last = len(CHUNKS) - 1
        banks0, list0 = score(0)
        s0 = empty(banks0[0][:], "s0")
        banks1, list1 = score(1)
        scatter(s0, 0, list0)
        banks2, list2 = score(2)
        s1_early = empty(banks1[0][:, 0:2, :], "g2_2")
        s1_late = empty(banks1[0][:, 2:4, :], "z_rows2")
        s2 = [empty(bank[:], "s2_%d" % i) for i, bank in enumerate(banks2)]
        scatter(s1_early, 0, list1)
        scatter(s1_late, 2, list1)

        w2_bf = slot([P, N, PACK], BF16, "g2_1")
        for mt in range(N // P):
            cols = slice(mt * P, (mt + 1) * P)
            nc.scalar.activation(
                w2_bf[:, cols, :].rearrange("p (c i) j -> p c j i", i=4), w2_raw[:, :, cols].rearrange("p j (c i) -> p c j i", i=4), COPY
            )
        w2_c = slot([P, N], U32, "z_bf2")
        w2_s = keep.tile([P, N], U8, name="w2_s", align_bytes=64)
        nc.vector.quantize_mx(w2_c[:].bitcast(FP8X4), w2_s[:], w2_bf[:].rearrange("p n j -> p (n j)"))

        for i, s_sb in enumerate(s2):
            scatter(s_sb, 2 * i, list2)

        parts = (slice(0, SPLIT), slice(SPLIT, U))
        z2_rows = [keep.tile([P, PACK, part.stop - part.start], BF16, name="z2_rows%d" % i) for i, part in enumerate(parts)]
        for t in range(PACK):
            for rows, part in zip(z2_rows, parts):
                if t == PACK - 1:
                    nc.vector.tensor_scalar(rows[:, t, :], page[t][:, part], gt_sb[:, t : t + 1], None, ALU.mult)
                else:
                    nc.scalar.activation(rows[:, t, :], page[t][:, part], COPY, scale=gt_sb[:, t : t + 1])

        start = 0
        pieces = []
        for wc, width in enumerate(WIDTHS):
            cols = slice(start, start + width)
            rows = z2_rows[0][:, :, cols] if start < SPLIT else z2_rows[1][:, :, start - SPLIT : start - SPLIT + width]
            start = start + width
            z2_bf = slot([P, width, PACK], BF16, "z2_bf%d" % wc)
            weave = nc.vector.tensor_copy if wc == 0 else nc.scalar.copy
            weave(z2_bf[:].rearrange("p (c i) t -> p c t i", i=4), rows.rearrange("p t (c i) -> p c t i", i=4))
            z2_c = keep.tile([P, width], U32, name="z2_c%d" % wc, align_bytes=64)
            z2_s = keep.tile([P, width], U8, name="z2_s%d" % wc, align_bytes=64)
            nc.vector.quantize_mx(z2_c[:].bitcast(FP8X4), z2_s[:], z2_bf[:].rearrange("p c t -> p (c t)"))
            pieces.append((cols, z2_c, z2_s))

        n_bank = 0
        for cols, z2_c, z2_s in pieces:
            width = cols.stop - cols.start
            per_bank = BANK // width
            for m0 in range(0, N // P, per_bank):
                bank = psum.tile([P, per_bank, width], F32, name="obank", tag="bank%d" % n_bank)
                for i in range(per_bank):
                    m_cols = slice((m0 + i) * P, (m0 + i + 1) * P)
                    nc.tensor.matmul_mx(bank[:, i, :], lhsT=w2_c[:, m_cols].bitcast(FP8X4), lhsT_scale=w2_s[:, m_cols],
                                        rhs=z2_c[:].bitcast(FP8X4), rhs_scale=z2_s[:], start=True, stop=True)
                o = slot([P, per_bank, width], F32, "z2_bf%d" % (n_bank + 1) if n_bank + 1 < len(WIDTHS) else "o%d" % n_bank)
                nc.vector.tensor_tensor(o[:], bank[:], res_sb[:, m0 : m0 + per_bank, cols], ALU.add)
                nc.sync.dma_start(out_rows[:, m0 : m0 + per_bank, cols], o[:])
                n_bank = n_bank + 1
